import numpy as np
import ml_dtypes


def mxq(x, axis, fmt="e4m3"):
    dtype, down = {"e4m3": (ml_dtypes.float8_e4m3fn, 7), "e5m2": (ml_dtypes.float8_e5m2, 14)}[fmt]
    v = np.moveaxis(np.asarray(x, np.float32).astype(ml_dtypes.bfloat16).astype(np.float64), axis, -1)
    blocks = v.reshape(v.shape[:-1] + (-1, 32))
    amax = np.abs(blocks).max(-1, keepdims=True)
    byte = np.maximum(np.where(amax > 0, np.frexp(amax)[1] - 1 + 127, 0) - down, 1)
    scale = np.exp2(byte - 127.0)
    codes = (blocks / scale).astype(np.float32).astype(dtype).astype(np.float64)
    return np.moveaxis((codes * scale).reshape(v.shape), -1, axis)


WIDE = False


def mx_kscale(k):
    if not WIDE:
        return np.ones(k)
    levels = np.array([30, -30])
    if k % 512:
        return np.exp2(np.random.permutation(np.resize(levels, k // 32))).repeat(32)
    a = np.empty((k // 512, 16))
    for p in range(k // 512):
        a[p, :8] = np.random.permutation(np.resize(levels, 8))
        for g in range(8):
            far = levels[np.abs(levels - a[p, g]) >= 10]
            a[p, g + 8] = far[np.random.randint(len(far))]
    return np.exp2(a.ravel()).repeat(32)


def f64(x):
    return np.asarray(x).astype(np.float64)


def striped(idx):
    return np.tile(np.asarray(idx).reshape(-1, 16).T, (8, 1)).astype(np.uint16)


def unstriped(offs):
    return offs[:16].T.reshape(-1).astype(np.int64)


E2M1 = np.array([0.0, 0.5, 1.0, 1.5, 2.0, 3.0, 4.0, 6.0, -0.0, -0.5, -1.0, -1.5, -2.0, -3.0, -4.0, -6.0])


def pack_weight(w, fmt):
    k, n = w.shape
    w = f64(np.asarray(w, np.float32).astype(ml_dtypes.bfloat16)).reshape(k // 32, 32, n)
    amax = np.abs(w).max(1)
    if fmt in ("e4m3", "e5m2"):
        byte = np.frexp(amax)[1] - 1 + 127 - (7 if fmt == "e4m3" else 14)
    else:
        mant, ex = np.frexp(amax / 6.0)
        byte = np.where(mant > 0.5, ex, ex - 1) + 127
    byte = np.clip(np.where(amax > 0, byte, 1), 1, 254)
    scaled = (w * np.exp2(127.0 - byte)[:, None, :]).reshape(k, n).astype(np.float32)
    by_word = np.ascontiguousarray(scaled.reshape(k // 512, 128, 4, n).transpose(0, 1, 3, 2))
    if fmt in ("e4m3", "e5m2"):
        words = by_word.astype(ml_dtypes.float8_e4m3fn if fmt == "e4m3" else ml_dtypes.float8_e5m2).view(np.uint8)
    else:
        c = by_word.astype(ml_dtypes.float4_e2m1fn).view(np.uint8) & 0xF
        words = (c[..., 0::2] | (c[..., 1::2] << 4)).reshape(k // 512, 128, 2 * n)
    return np.ascontiguousarray(words), np.ascontiguousarray(byte.astype(np.uint8).reshape(k // 512, 16, n))


def unpack_weight(words, scales, fmt):
    g, _, n = scales.shape
    words = np.ascontiguousarray(words).reshape(g, 128, n, -1)
    if fmt in ("e4m3", "e5m2"):
        vals = words.view(ml_dtypes.float8_e4m3fn if fmt == "e4m3" else ml_dtypes.float8_e5m2).astype(np.float64)
    else:
        nib = np.empty((g, 128, n, 4), np.uint8)
        nib[..., 0::2] = words & 0xF
        nib[..., 1::2] = words >> 4
        vals = E2M1[nib]
    vals = vals * np.repeat(np.exp2(scales.astype(np.float64) - 127.0), 8, axis=1)[..., None]
    return vals.transpose(0, 1, 3, 2).reshape(g * 512, n)


K, T, J, S, R, N = 1024, 1024, 256, 512, 512, 256


def setup_inputs():
    n = np.random.standard_normal
    idx = np.random.permutation(T)[:J]
    idx2 = np.random.permutation(S)[:J]
    fk = mx_kscale(K)
    fr = mx_kscale(R)
    wp = pack_weight(n((K, R)) * 1 / np.sqrt(K) * fk[:, None] * fr, "e5m2")
    wbp = pack_weight(n((R, N)) * 1 / np.sqrt(R) / fr[:, None], "e2m1")
    return {
        "xa": (n((K, T))).astype(np.float32),
        "xb": (n((K, S))).astype(np.float32),
        "fk": (np.random.uniform(0.5, 2.0, (K, 1)) / fk[:, None]).astype(np.float32),
        "w_words": wp[0],
        "w_scales": wp[1],
        "us": (np.random.uniform(0.5, 2.0, (R, 1)) * fr[:, None]).astype(np.float32),
        "wb_words": wbp[0],
        "wb_scales": wbp[1],
        "bi": (np.random.uniform(-0.5, 0.5, (1, N))).astype(np.float32),
        "offs": striped(idx),
        "offs2": striped(idx2),
    }


def reference(xa, xb, fk, w_words, w_scales, us, wb_words, wb_scales, bi, offs, offs2):
    idx = unstriped(offs)
    idx2 = unstriped(offs2)
    wu = unpack_weight(w_words, w_scales, "e5m2")
    wbu = unpack_weight(wb_words, wb_scales, "e2m1")
    u = f64(xa)[:, idx] * f64(xb)[:, idx2] * f64(fk)
    uq = mxq(u, 0, "e5m2")
    a = wu.T @ uq
    pk1 = np.max(np.abs(a), axis=1, keepdims=True)
    hid = a / pk1 * f64(us)
    hidq = mxq(hid, 0, "e5m2")
    p = hidq.T @ wbu
    ea = np.exp(0.7 * p + f64(bi))
    y = 256.0 * ea / np.sum(ea, axis=1, keepdims=True)
    return y

@@ -1,0 +1,231 @@
+from contextlib import ExitStack
+
+import concourse.mybir as mybir
+from concourse.masks import make_identity
+
+K, T, J, S, R, N = 1024, 1024, 256, 512, 512, 256
+FLOPS = 2 * K * R * J + 2 * R * J * N
+
+F32 = mybir.dt.float32
+BF16 = mybir.dt.bfloat16
+I32 = mybir.dt.int32
+U16 = mybir.dt.uint16
+U8 = mybir.dt.uint8
+E5M2X4 = mybir.dt.float8_e5m2_x4
+E2M1X4 = mybir.dt.float4_e2m1fn_x4
+ALU = mybir.AluOpType
+ACT = mybir.ActivationFunctionType
+AXIS_X = mybir.AxisListType.X
+
+P = 128
+PACK = 4
+PASSES = K // (P * PACK)
+HALF = J // 2
+LIST_COLS = J // 16
+
+
+def tile_list_entryproducts_peakscaled_rowshares_kernel(
+    tc, xa, xb, fk, w_words, w_scales, us, wb_words, wb_scales, bi, offs, offs2, out
+):
+    nc = tc.nc
+    with ExitStack() as ctx:
+        keep = ctx.enter_context(tc.tile_pool(name="keep", bufs=1))
+        psum = ctx.enter_context(tc.psum_pool(name="psum", bufs=1))
+
+        list_a = keep.tile([P, LIST_COLS], U16, name="list_a")
+        list_b = keep.tile([P, LIST_COLS], U16, name="list_b")
+        fk_sb = keep.tile([P, PASSES, PACK], F32, name="fk_sb")
+        us_sb = keep.tile([P, PACK], F32, name="us_sb")
+        bi_col = keep.tile([P, 2], F32, name="bi_col")
+        w_raw = keep.tile([P, PASSES, R], I32, name="w_raw")
+        ws_raw = keep.tile([P, PASSES, R], U8, name="ws_raw")
+        wb_codes = keep.tile([P, 2 * N], U8, name="wb_codes", align_bytes=64)
+        wb_plane = keep.tile([P, N], U8, name="wb_plane", align_bytes=64)
+        xb_sb = [keep.tile([P, PACK, S], F32, name="xb_sb%d" % a) for a in range(PASSES)]
+        xa_loads = [(0, 0, 2), (0, 2, 4), (1, 0, 2), (1, 2, 3), (1, 3, 4)]
+        xa_sb = [keep.tile([P, t1 - t0, T], F32, name="xa_sb%d" % g) for g, (a, t0, t1) in enumerate(xa_loads)]
+
+        xa_rows = xa.rearrange("(a p t) c -> a p t c", a=PASSES, t=PACK)
+        xb_rows = xb.rearrange("(a p t) c -> a p t c", a=PASSES, t=PACK)
+        ws_rows = w_scales.bitcast(I32).rearrange("a (q r) c -> r q a c", r=4)
+        wbs_rows = wb_scales[0].bitcast(I32).rearrange("(q r) c -> r q c", r=4)
+
+        nc.vector.memset(ws_raw[:].rearrange("p a c -> p (a c)").bitcast(I32), 0)
+        nc.vector.memset(wb_plane[:].bitcast(I32), 0)
+
+        def load_xa(g):
+            a, t0, t1 = xa_loads[g]
+            nc.sync.dma_start(out=xa_sb[g][:], in_=xa_rows[a, :, t0:t1, :])
+
+        def load_w_scales(r):
+            nc.sync.dma_start(out=ws_raw[:].bitcast(I32)[r:P:32, :, :], in_=ws_rows[r])
+
+        def load_wb_scales(r):
+            nc.sync.dma_start(out=wb_plane[:].bitcast(I32)[r:P:32, :], in_=wbs_rows[r])
+
+        nc.sync.dma_start(out=xb_sb[0][:], in_=xb_rows[0])
+        nc.sync.dma_start(list_b[:], offs2)
+        nc.sync.dma_start(out=w_raw[:], in_=w_words.rearrange("a p c t -> p a (c t)").bitcast(I32))
+        nc.sync.dma_start(out=xb_sb[1][:], in_=xb_rows[1])
+        nc.sync.dma_start(list_a[:], offs)
+        nc.sync.dma_start(out=fk_sb[:], in_=fk.rearrange("(a p t) o -> p a (t o)", a=PASSES, t=PACK))
+        load_xa(0)
+        for r in range(4):
+            load_w_scales(r)
+        load_xa(1)
+        nc.sync.dma_start(out=us_sb[:], in_=us.rearrange("(p t) o -> p (t o)", t=PACK))
+        nc.sync.dma_start(out=bi_col[:], in_=bi.rearrange("o (p h) -> p (o h)", h=2))
+        load_xa(2)
+        nc.sync.dma_start(out=wb_codes[:].bitcast(I32), in_=wb_words[0].bitcast(I32))
+        for r in range(3):
+            load_wb_scales(r)
+        load_xa(3)
+        load_wb_scales(3)
+        load_xa(4)
+
+        picked_a = [keep.tile([P, PACK, J], F32, name="picked_a%d" % a) for a in range(PASSES)]
+        picked_b = [keep.tile([P, PACK, J], F32, name="picked_b%d" % a) for a in range(PASSES)]
+        u_rows = [keep.tile([P, PACK, J], F32, name="u_rows%d" % a) for a in range(PASSES)]
+        u_bf = [keep.tile([P, J, PACK], BF16, name="u_bf%d" % a, align_bytes=64) for a in range(PASSES)]
+        u_codes = [keep.tile([P, J], I32, name="u_codes%d" % a, align_bytes=64) for a in range(PASSES)]
+        u_plane = [keep.tile([P, J], U8, name="u_plane%d" % a, align_bytes=64) for a in range(PASSES)]
+        w_codes = keep.tile([P, PASSES, PACK, P], I32, name="w_codes", align_bytes=64)
+        w_plane = keep.tile([P, PASSES, PACK, P], U8, name="w_plane", align_bytes=64)
+
+        for t in range(PACK):
+            nc.vector.tensor_copy(picked_b[0][:, t, :], xb_sb[0][:, t, :].indirect(list_b[:]))
+        for a in range(PASSES):
+            nc.vector.tensor_copy(
+                out=w_codes[:, a].rearrange("p t (c i) -> p c t i", i=4),
+                in_=w_raw[:, a].rearrange("p (c i t) -> p c t i", i=4, t=PACK),
+            )
+        for t in range(PACK):
+            nc.vector.tensor_copy(picked_b[1][:, t, :], xb_sb[1][:, t, :].indirect(list_b[:]))
+        for a in range(PASSES):
+            nc.vector.tensor_copy(
+                out=w_plane[:, a].rearrange("p t (c i) -> p c t i", i=16),
+                in_=ws_raw[:, a].rearrange("p (c i t) -> p c t i", i=16, t=PACK),
+            )
+
+        ident = keep.tile([P, P], F32, name="ident")
+        make_identity(nc, ident[:])
+        bi_ps = psum.tile([P, 2, P], F32, name="bi_ps")
+        for h in range(2):
+            nc.tensor.transpose(bi_ps[:, h, :], bi_col[:, h : h + 1].to_broadcast([P, P]), ident[:])
+        bi_rows = keep.tile([P, N], F32, name="bi_rows")
+        nc.scalar.copy(bi_rows[:].rearrange("p (c h) -> p c h", h=2), bi_ps[:].rearrange("p h c -> p c h"))
+
+        a_ps = [psum.tile([P, J], F32, name="a_ps%d" % t) for t in range(PACK)]
+
+        def multiply(a, t, cols):
+            nc.vector.scalar_tensor_tensor(
+                out=u_rows[a][:, t, cols],
+                in0=picked_a[a][:, t, cols],
+                scalar=fk_sb[:, a, t : t + 1],
+                in1=picked_b[a][:, t, cols],
+                op0=ALU.mult,
+                op1=ALU.mult,
+            )
+
+        def interleave(a, cols):
+            nc.vector.tensor_copy(
+                out=u_bf[a][:, cols, :].rearrange("p (c i) t -> p c t i", i=4),
+                in_=u_rows[a][:, :, cols].rearrange("p t (c i) -> p c t i", i=4),
+            )
+
+        def quantize(a, cols):
+            nc.vector.quantize_mx(
+                out=u_codes[a][:, cols].bitcast(E5M2X4),
+                scales=u_plane[a][:, cols],
+                in_=u_bf[a][:, cols, :].rearrange("p c t -> p (c t)"),
+            )
+
+        def first_product(a):
+            for t in range(PACK):
+                nc.tensor.matmul_mx(
+                    out=a_ps[t][:],
+                    lhsT=w_codes[:, a, t, :].bitcast(E5M2X4),
+                    lhsT_scale=w_plane[:, a, t, :],
+                    rhs=u_codes[a][:].bitcast(E5M2X4),
+                    rhs_scale=u_plane[a][:],
+                    start=(a == 0),
+                    stop=(a == PASSES - 1),
+                )
+
+        halves = [slice(0, HALF), slice(HALF, J)]
+        everything = slice(0, J)
+        for g, (a, t0, t1) in enumerate(xa_loads[:-1]):
+            for t in range(t0, t1):
+                nc.scalar.activation(picked_a[a][:, t, :], xa_sb[g][:, t - t0, :].indirect(list_a[:]), ACT.Copy)
+                multiply(a, t, everything)
+            if t1 == PACK:
+                interleave(a, everything)
+                quantize(a, everything)
+                first_product(a)
+
+        a, t = PASSES - 1, PACK - 1
+        last = xa_sb[-1][:, 0, :]
+        nc.scalar.activation(picked_a[a][:, t, halves[1]], last.indirect(list_a[:, LIST_COLS // 2 :]), ACT.Copy)
+        nc.vector.tensor_copy(picked_a[a][:, t, halves[0]], last.indirect(list_a[:, : LIST_COLS // 2]))
+        for step in (lambda cols: multiply(a, t, cols), lambda cols: interleave(a, cols), lambda cols: quantize(a, cols)):
+            for cols in halves:
+                step(cols)
+        first_product(a)
+
+        a_sb = keep.tile([P, PACK, J], F32, name="a_sb")
+        peak = keep.tile([P, PACK], F32, name="peak")
+        inv_peak = keep.tile([P, PACK], F32, name="inv_peak")
+        factor = keep.tile([P, PACK], F32, name="factor")
+        for t in range(PACK):
+            nc.scalar.copy(a_sb[:, t, :], a_ps[t][:])
+            nc.vector.tensor_reduce(peak[:, t : t + 1], a_sb[:, t, :], AXIS_X, ALU.max, apply_absolute_value=True)
+        nc.vector.reciprocal(inv_peak[:], peak[:])
+        nc.vector.tensor_tensor(factor[:], inv_peak[:], us_sb[:], ALU.mult)
+
+        hid_bf = [keep.tile([P, HALF, PACK], BF16, name="hid_bf%d" % h, align_bytes=64) for h in range(2)]
+        hid_codes = [keep.tile([P, HALF], I32, name="hid_codes%d" % h, align_bytes=64) for h in range(2)]
+        hid_plane = [keep.tile([P, HALF], U8, name="hid_plane%d" % h, align_bytes=64) for h in range(2)]
+        p_ps = [psum.tile([P, N], F32, name="p_ps%d" % h) for h in range(2)]
+        factor_spread = factor[:].rearrange("p (c t i) -> p c t i", c=1, i=1).to_broadcast([P, HALF // 4, PACK, 4])
+        for h in range(2):
+            nc.vector.tensor_tensor(
+                hid_bf[h][:].rearrange("p (c i) t -> p c t i", i=4),
+                a_sb[:, :, halves[h]].rearrange("p t (c i) -> p c t i", i=4),
+                factor_spread,
+                ALU.mult,
+            )
+        for h in range(2):
+            nc.vector.quantize_mx(
+                out=hid_codes[h][:].bitcast(E5M2X4),
+                scales=hid_plane[h][:],
+                in_=hid_bf[h][:].rearrange("p c t -> p (c t)"),
+            )
+            nc.tensor.matmul_mx(
+                out=p_ps[h][:],
+                lhsT=hid_codes[h][:].bitcast(E5M2X4),
+                lhsT_scale=hid_plane[h][:],
+                rhs=wb_codes[:].bitcast(E2M1X4),
+                rhs_scale=wb_plane[:],
+                start=True,
+                stop=True,
+            )
+
+        neg_z = [keep.tile([P, N], F32, name="neg_z%d" % h) for h in range(2)]
+        neg_top = [keep.tile([P, 1], F32, name="neg_top%d" % h) for h in range(2)]
+        ea = [keep.tile([P, N], F32, name="ea%d" % h) for h in range(2)]
+        total = [keep.tile([P, 1], F32, name="total%d" % h) for h in range(2)]
+        inv_total = [keep.tile([P, 1], F32, name="inv_total%d" % h) for h in range(2)]
+        shares = [keep.tile([P, N], F32, name="shares%d" % h) for h in range(2)]
+        for h in range(2):
+            nc.vector.scalar_tensor_tensor(
+                out=neg_z[h][:], in0=p_ps[h][:], scalar=-0.7, in1=bi_rows[:], op0=ALU.mult, op1=ALU.subtract
+            )
+        for h in range(2):
+            nc.vector.tensor_reduce(neg_top[h][:], neg_z[h][:], AXIS_X, ALU.min)
+            nc.scalar.activation(
+                ea[h][:], neg_z[h][:], ACT.Exp, bias=neg_top[h][:], scale=-1.0, accum_out=total[h][:]
+            )
+        for h in range(2):
+            nc.vector.reciprocal(inv_total[h][:], total[h][:])
+            nc.vector.tensor_scalar(shares[h][:], ea[h][:], inv_total[h][:], 256.0, ALU.mult, ALU.mult)
+            nc.sync.dma_start(out=out[halves[h], :], in_=shares[h][:])

@@ -37,13 +37,14 @@ def tile_list_entryproducts_peakscaled_rowshares_kernel(
         fk_sb = keep.tile([P, PASSES, PACK], F32, name="fk_sb")
         us_sb = keep.tile([P, PACK], F32, name="us_sb")
         bi_col = keep.tile([P, 2], F32, name="bi_col")
-        w_raw = keep.tile([P, PASSES, R], I32, name="w_raw")
+        w_raw = [keep.tile([P, R], I32, name="w_raw%d" % a) for a in range(PASSES)]
         ws_raw = keep.tile([P, PASSES, R], U8, name="ws_raw")
         wb_codes = keep.tile([P, 2 * N], U8, name="wb_codes", align_bytes=64)
         wb_plane = keep.tile([P, N], U8, name="wb_plane", align_bytes=64)
         xb_sb = [keep.tile([P, PACK, S], F32, name="xb_sb%d" % a) for a in range(PASSES)]
-        xa_loads = [(0, 0, 2), (0, 2, 4), (1, 0, 2), (1, 2, 3), (1, 3, 4)]
+        xa_loads = [(0, 0, 2), (0, 2, 4), (1, 0, 2), (1, 2, 3)]
         xa_sb = [keep.tile([P, t1 - t0, T], F32, name="xa_sb%d" % g) for g, (a, t0, t1) in enumerate(xa_loads)]
+        xa_last = keep.tile([P, T], F32, name="xa_last")
 
         xa_rows = xa.rearrange("(a p t) c -> a p t c", a=PASSES, t=PACK)
         xb_rows = xb.rearrange("(a p t) c -> a p t c", a=PASSES, t=PACK)
@@ -60,47 +61,44 @@ def tile_list_entryproducts_peakscaled_rowshares_kernel(
         def load_w_scales(r):
             nc.sync.dma_start(out=ws_raw[:].bitcast(I32)[r:P:32, :, :], in_=ws_rows[r])
 
+        def load_w_words(a):
+            nc.sync.dma_start(out=w_raw[a][:], in_=w_words[a].rearrange("p c t -> p (c t)").bitcast(I32))
+
         def load_wb_scales(r):
             nc.sync.dma_start(out=wb_plane[:].bitcast(I32)[r:P:32, :], in_=wbs_rows[r])
 
         nc.sync.dma_start(out=xb_sb[0][:], in_=xb_rows[0])
         nc.sync.dma_start(list_b[:], offs2)
-        nc.sync.dma_start(out=w_raw[:], in_=w_words.rearrange("a p c t -> p a (c t)").bitcast(I32))
-        nc.sync.dma_start(out=xb_sb[1][:], in_=xb_rows[1])
+        nc.sync.dma_start(out=bi_col[:], in_=bi.rearrange("o (p h) -> p (o h)", h=2))
         nc.sync.dma_start(list_a[:], offs)
-        nc.sync.dma_start(out=fk_sb[:], in_=fk.rearrange("(a p t) o -> p a (t o)", a=PASSES, t=PACK))
         load_xa(0)
+        nc.sync.dma_start(out=fk_sb[:], in_=fk.rearrange("(a p t) o -> p a (t o)", a=PASSES, t=PACK))
+        load_xa(1)
+        load_w_words(0)
         for r in range(4):
             load_w_scales(r)
-        load_xa(1)
+        nc.sync.dma_start(out=xb_sb[1][:], in_=xb_rows[1])
         nc.sync.dma_start(out=us_sb[:], in_=us.rearrange("(p t) o -> p (t o)", t=PACK))
-        nc.sync.dma_start(out=bi_col[:], in_=bi.rearrange("o (p h) -> p (o h)", h=2))
         load_xa(2)
-        nc.sync.dma_start(out=wb_codes[:].bitcast(I32), in_=wb_words[0].bitcast(I32))
-        for r in range(3):
+        for r in range(4):
             load_wb_scales(r)
         load_xa(3)
-        load_wb_scales(3)
-        load_xa(4)
+        nc.sync.dma_start(out=xa_last[:], in_=xa_rows[PASSES - 1, :, PACK - 1, :])
+        load_w_words(1)
+        nc.sync.dma_start(out=wb_codes[:].bitcast(I32), in_=wb_words[0].bitcast(I32))
 
-        picked_a = [keep.tile([P, PACK, J], F32, name="picked_a%d" % a) for a in range(PASSES)]
+        picked_a = [keep.tile([P, PACK - a, J], F32, name="picked_a%d" % a) for a in range(PASSES)]
         picked_b = [keep.tile([P, PACK, J], F32, name="picked_b%d" % a) for a in range(PASSES)]
-        u_rows = [keep.tile([P, PACK, J], F32, name="u_rows%d" % a) for a in range(PASSES)]
-        u_bf = [keep.tile([P, J, PACK], BF16, name="u_bf%d" % a, align_bytes=64) for a in range(PASSES)]
+        u_rows = [keep.tile([P, PACK, J], F32, name="u_rows0")]
+        u_bf = keep.tile([P, J, PACK], BF16, name="u_bf", tag="u_bf", align_bytes=64)
+        scaled_b = keep.tile([P, J], F32, name="scaled_b", tag="scaled_b", align_bytes=64)
         u_codes = [keep.tile([P, J], I32, name="u_codes%d" % a, align_bytes=64) for a in range(PASSES)]
         u_plane = [keep.tile([P, J], U8, name="u_plane%d" % a, align_bytes=64) for a in range(PASSES)]
-        w_codes = keep.tile([P, PASSES, PACK, P], I32, name="w_codes", align_bytes=64)
+        w_codes = {}
         w_plane = keep.tile([P, PASSES, PACK, P], U8, name="w_plane", align_bytes=64)
 
         for t in range(PACK):
             nc.vector.tensor_copy(picked_b[0][:, t, :], xb_sb[0][:, t, :].indirect(list_b[:]))
-        for a in range(PASSES):
-            nc.vector.tensor_copy(
-                out=w_codes[:, a].rearrange("p t (c i) -> p c t i", i=4),
-                in_=w_raw[:, a].rearrange("p (c i t) -> p c t i", i=4, t=PACK),
-            )
-        for t in range(PACK):
-            nc.vector.tensor_copy(picked_b[1][:, t, :], xb_sb[1][:, t, :].indirect(list_b[:]))
         for a in range(PASSES):
             nc.vector.tensor_copy(
                 out=w_plane[:, a].rearrange("p t (c i) -> p c t i", i=16),
@@ -127,24 +125,33 @@ def tile_list_entryproducts_peakscaled_rowshares_kernel(
                 op1=ALU.mult,
             )
 
-        def interleave(a, cols):
-            nc.vector.tensor_copy(
-                out=u_bf[a][:, cols, :].rearrange("p (c i) t -> p c t i", i=4),
-                in_=u_rows[a][:, :, cols].rearrange("p t (c i) -> p c t i", i=4),
+        def interleave(copy, dst, a, cols):
+            copy(
+                dst[:].rearrange("p (c i) t -> p c t i", i=4),
+                u_rows[a][:, :, cols].rearrange("p t (c i) -> p c t i", i=4),
             )
 
-        def quantize(a, cols):
+        def quantize(src, a, cols):
             nc.vector.quantize_mx(
                 out=u_codes[a][:, cols].bitcast(E5M2X4),
                 scales=u_plane[a][:, cols],
-                in_=u_bf[a][:, cols, :].rearrange("p c t -> p (c t)"),
+                in_=src[:].rearrange("p c t -> p (c t)"),
+            )
+
+        def deal_w(a, t0, t1, tag):
+            dealt = keep.tile([P, t1 - t0, P], I32, name="w_codes%d%d" % (a, t0), tag=tag, align_bytes=64)
+            for t in range(t0, t1):
+                w_codes[a, t] = dealt[:, t - t0, :]
+            nc.vector.tensor_copy(
+                out=dealt[:].rearrange("p t (c i) -> p c t i", i=4),
+                in_=w_raw[a][:].rearrange("p (c i t) -> p c t i", i=4, t=PACK)[:, :, t0:t1, :],
             )
 
         def first_product(a):
             for t in range(PACK):
                 nc.tensor.matmul_mx(
                     out=a_ps[t][:],
-                    lhsT=w_codes[:, a, t, :].bitcast(E5M2X4),
+                    lhsT=w_codes[a, t].bitcast(E5M2X4),
                     lhsT_scale=w_plane[:, a, t, :],
                     rhs=u_codes[a][:].bitcast(E5M2X4),
                     rhs_scale=u_plane[a][:],
@@ -154,22 +161,36 @@ def tile_list_entryproducts_peakscaled_rowshares_kernel(
 
         halves = [slice(0, HALF), slice(HALF, J)]
         everything = slice(0, J)
-        for g, (a, t0, t1) in enumerate(xa_loads[:-1]):
+        for g, (a, t0, t1) in enumerate(xa_loads):
             for t in range(t0, t1):
                 nc.scalar.activation(picked_a[a][:, t, :], xa_sb[g][:, t - t0, :].indirect(list_a[:]), ACT.Copy)
                 multiply(a, t, everything)
             if t1 == PACK:
-                interleave(a, everything)
-                quantize(a, everything)
+                interleave(nc.vector.tensor_copy, u_bf, a, everything)
+                deal_w(a, 0, PACK, "w_codes")
+                quantize(u_bf, a, everything)
                 first_product(a)
+                u_rows.append(keep.tile([P, PACK, J], F32, name="u_rows1", tag="u_bf", align_bytes=64))
+                for t in range(0, 2):
+                    nc.scalar.activation(picked_b[1][:, t, :], xb_sb[1][:, t, :].indirect(list_b[:]), ACT.Copy)
+                for t in range(2, PACK):
+                    nc.vector.tensor_copy(picked_b[1][:, t, :], xb_sb[1][:, t, :].indirect(list_b[:]))
+                nc.vector.tensor_scalar(scaled_b[:], picked_b[1][:, PACK - 1, :], fk_sb[:, 1, PACK - 1 : PACK], None, ALU.mult)
 
         a, t = PASSES - 1, PACK - 1
-        last = xa_sb[-1][:, 0, :]
-        nc.scalar.activation(picked_a[a][:, t, halves[1]], last.indirect(list_a[:, LIST_COLS // 2 :]), ACT.Copy)
-        nc.vector.tensor_copy(picked_a[a][:, t, halves[0]], last.indirect(list_a[:, : LIST_COLS // 2]))
-        for step in (lambda cols: multiply(a, t, cols), lambda cols: interleave(a, cols), lambda cols: quantize(a, cols)):
-            for cols in halves:
-                step(cols)
+        picked_last = keep.tile([P, HALF], F32, name="picked_last")
+        nc.scalar.activation(picked_last[:], xa_last[:].indirect(list_a[:, LIST_COLS // 2 :]), ACT.Copy)
+        nc.vector.tensor_tensor(
+            u_rows[a][:, t, halves[0]], xa_last[:].indirect(list_a[:, : LIST_COLS // 2]), scaled_b[:, halves[0]], ALU.mult
+        )
+        nc.vector.tensor_tensor(u_rows[a][:, t, halves[1]], picked_last[:], scaled_b[:, halves[1]], ALU.mult)
+        u_bf_half = [keep.tile([P, HALF, PACK], BF16, name="u_bf_half%d" % h, tag="u_bf_half%d" % h, align_bytes=64) for h in range(2)]
+        interleave(nc.scalar.copy, u_bf_half[0], a, halves[0])
+        deal_w(a, 0, 2, "scaled_b")
+        interleave(nc.vector.tensor_copy, u_bf_half[1], a, halves[1])
+        for h in range(2):
+            quantize(u_bf_half[h], a, halves[h])
+        deal_w(a, 2, PACK, "u_bf_half0")
         first_product(a)
 
         a_sb = keep.tile([P, PACK, J], F32, name="a_sb")

@@ -68,24 +68,24 @@ def tile_list_entryproducts_peakscaled_rowshares_kernel(
             nc.sync.dma_start(out=wb_plane[:].bitcast(I32)[r:P:32, :], in_=wbs_rows[r])
 
         nc.sync.dma_start(out=xb_sb[0][:], in_=xb_rows[0])
+        nc.scalar.dma_start(out=bi_col[:], in_=bi.rearrange("o (p h) -> p (o h)", h=2))
+        nc.scalar.dma_start(out=fk_sb[:], in_=fk.rearrange("(a p t) o -> p a (t o)", a=PASSES, t=PACK))
         nc.sync.dma_start(list_b[:], offs2)
-        nc.sync.dma_start(out=bi_col[:], in_=bi.rearrange("o (p h) -> p (o h)", h=2))
-        nc.sync.dma_start(list_a[:], offs)
         load_xa(0)
-        nc.sync.dma_start(out=fk_sb[:], in_=fk.rearrange("(a p t) o -> p a (t o)", a=PASSES, t=PACK))
+        nc.sync.dma_start(list_a[:], offs)
         load_xa(1)
         load_w_words(0)
         for r in range(4):
             load_w_scales(r)
         nc.sync.dma_start(out=xb_sb[1][:], in_=xb_rows[1])
-        nc.sync.dma_start(out=us_sb[:], in_=us.rearrange("(p t) o -> p (t o)", t=PACK))
         load_xa(2)
-        for r in range(4):
-            load_wb_scales(r)
         load_xa(3)
         nc.sync.dma_start(out=xa_last[:], in_=xa_rows[PASSES - 1, :, PACK - 1, :])
         load_w_words(1)
+        nc.sync.dma_start(out=us_sb[:], in_=us.rearrange("(p t) o -> p (t o)", t=PACK))
         nc.sync.dma_start(out=wb_codes[:].bitcast(I32), in_=wb_words[0].bitcast(I32))
+        for r in range(4):
+            load_wb_scales(r)
 
         picked_a = [keep.tile([P, PACK - a, J], F32, name="picked_a%d" % a) for a in range(PASSES)]
         picked_b = [keep.tile([P, PACK, J], F32, name="picked_b%d" % a) for a in range(PASSES)]

@@ -42,7 +42,7 @@ def tile_list_entryproducts_peakscaled_rowshares_kernel(
         wb_codes = keep.tile([P, 2 * N], U8, name="wb_codes", align_bytes=64)
         wb_plane = keep.tile([P, N], U8, name="wb_plane", align_bytes=64)
         xb_sb = [keep.tile([P, PACK, S], F32, name="xb_sb%d" % a) for a in range(PASSES)]
-        xa_loads = [(0, 0, 2), (0, 2, 4), (1, 0, 2), (1, 2, 3)]
+        xa_loads = [(0, 0, 2), (0, 2, 4), (1, 0, 1), (1, 1, 2), (1, 2, 3)]
         xa_sb = [keep.tile([P, t1 - t0, T], F32, name="xa_sb%d" % g) for g, (a, t0, t1) in enumerate(xa_loads)]
         xa_last = keep.tile([P, T], F32, name="xa_last")
 
@@ -73,13 +73,14 @@ def tile_list_entryproducts_peakscaled_rowshares_kernel(
         nc.sync.dma_start(list_b[:], offs2)
         load_xa(0)
         nc.sync.dma_start(list_a[:], offs)
-        load_xa(1)
-        load_w_words(0)
         for r in range(4):
             load_w_scales(r)
+        load_xa(1)
+        load_w_words(0)
         nc.sync.dma_start(out=xb_sb[1][:], in_=xb_rows[1])
         load_xa(2)
         load_xa(3)
+        load_xa(4)
         nc.sync.dma_start(out=xa_last[:], in_=xa_rows[PASSES - 1, :, PACK - 1, :])
         load_w_words(1)
         nc.sync.dma_start(out=us_sb[:], in_=us.rearrange("(p t) o -> p (t o)", t=PACK))

from contextlib import ExitStack

import concourse.mybir as mybir
from concourse.masks import make_identity

K, T, J, S, R, N = 1024, 1024, 256, 512, 512, 256
FLOPS = 2 * K * R * J + 2 * R * J * N

F32 = mybir.dt.float32
BF16 = mybir.dt.bfloat16
I32 = mybir.dt.int32
U16 = mybir.dt.uint16
U8 = mybir.dt.uint8
E5M2X4 = mybir.dt.float8_e5m2_x4
E2M1X4 = mybir.dt.float4_e2m1fn_x4
ALU = mybir.AluOpType
ACT = mybir.ActivationFunctionType
AXIS_X = mybir.AxisListType.X

P = 128
PACK = 4
PASSES = K // (P * PACK)
HALF = J // 2
LIST_COLS = J // 16


def tile_list_entryproducts_peakscaled_rowshares_kernel(
    tc, xa, xb, fk, w_words, w_scales, us, wb_words, wb_scales, bi, offs, offs2, out
):
    nc = tc.nc
    with ExitStack() as ctx:
        keep = ctx.enter_context(tc.tile_pool(name="keep", bufs=1))
        psum = ctx.enter_context(tc.psum_pool(name="psum", bufs=1))

        list_a = keep.tile([P, LIST_COLS], U16, name="list_a")
        list_b = keep.tile([P, LIST_COLS], U16, name="list_b")
        fk_sb = keep.tile([P, PASSES, PACK], F32, name="fk_sb")
        us_sb = keep.tile([P, PACK], F32, name="us_sb")
        bi_col = keep.tile([P, 2], F32, name="bi_col")
        w_raw = [keep.tile([P, R], I32, name="w_raw%d" % a) for a in range(PASSES)]
        ws_raw = keep.tile([P, PASSES, R], U8, name="ws_raw")
        wb_codes = keep.tile([P, 2 * N], U8, name="wb_codes", align_bytes=64)
        wb_plane = keep.tile([P, N], U8, name="wb_plane", align_bytes=64)
        xb_sb = [keep.tile([P, PACK, S], F32, name="xb_sb%d" % a) for a in range(PASSES)]
        xa_loads = [(0, 0, 2), (0, 2, 4), (1, 0, 1), (1, 1, 2), (1, 2, 3)]
        xa_sb = [keep.tile([P, t1 - t0, T], F32, name="xa_sb%d" % g) for g, (a, t0, t1) in enumerate(xa_loads)]
        xa_last = keep.tile([P, T], F32, name="xa_last")

        xa_rows = xa.rearrange("(a p t) c -> a p t c", a=PASSES, t=PACK)
        xb_rows = xb.rearrange("(a p t) c -> a p t c", a=PASSES, t=PACK)
        ws_rows = w_scales.bitcast(I32).rearrange("a (q r) c -> r q a c", r=4)
        wbs_rows = wb_scales[0].bitcast(I32).rearrange("(q r) c -> r q c", r=4)

        nc.vector.memset(ws_raw[:].rearrange("p a c -> p (a c)").bitcast(I32), 0)
        nc.vector.memset(wb_plane[:].bitcast(I32), 0)

        def load_xa(g):
            a, t0, t1 = xa_loads[g]
            nc.sync.dma_start(out=xa_sb[g][:], in_=xa_rows[a, :, t0:t1, :])

        def load_w_scales(r):
            nc.sync.dma_start(out=ws_raw[:].bitcast(I32)[r:P:32, :, :], in_=ws_rows[r])

        def load_w_words(a):
            nc.sync.dma_start(out=w_raw[a][:], in_=w_words[a].rearrange("p c t -> p (c t)").bitcast(I32))

        def load_wb_scales(r):
            nc.sync.dma_start(out=wb_plane[:].bitcast(I32)[r:P:32, :], in_=wbs_rows[r])

        nc.sync.dma_start(out=xb_sb[0][:], in_=xb_rows[0])
        nc.scalar.dma_start(out=bi_col[:], in_=bi.rearrange("o (p h) -> p (o h)", h=2))
        nc.scalar.dma_start(out=fk_sb[:], in_=fk.rearrange("(a p t) o -> p a (t o)", a=PASSES, t=PACK))
        nc.sync.dma_start(list_b[:], offs2)
        load_xa(0)
        nc.sync.dma_start(list_a[:], offs)
        for r in range(4):
            load_w_scales(r)
        load_xa(1)
        load_w_words(0)
        nc.sync.dma_start(out=xb_sb[1][:], in_=xb_rows[1])
        load_xa(2)
        load_xa(3)
        load_xa(4)
        nc.sync.dma_start(out=xa_last[:], in_=xa_rows[PASSES - 1, :, PACK - 1, :])
        load_w_words(1)
        nc.sync.dma_start(out=us_sb[:], in_=us.rearrange("(p t) o -> p (t o)", t=PACK))
        nc.sync.dma_start(out=wb_codes[:].bitcast(I32), in_=wb_words[0].bitcast(I32))
        for r in range(4):
            load_wb_scales(r)

        picked_a = [keep.tile([P, PACK - a, J], F32, name="picked_a%d" % a) for a in range(PASSES)]
        picked_b = [keep.tile([P, PACK, J], F32, name="picked_b%d" % a) for a in range(PASSES)]
        u_rows = [keep.tile([P, PACK, J], F32, name="u_rows0")]
        u_bf = keep.tile([P, J, PACK], BF16, name="u_bf", tag="u_bf", align_bytes=64)
        scaled_b = keep.tile([P, J], F32, name="scaled_b", tag="scaled_b", align_bytes=64)
        u_codes = [keep.tile([P, J], I32, name="u_codes%d" % a, align_bytes=64) for a in range(PASSES)]
        u_plane = [keep.tile([P, J], U8, name="u_plane%d" % a, align_bytes=64) for a in range(PASSES)]
        w_codes = {}
        w_plane = keep.tile([P, PASSES, PACK, P], U8, name="w_plane", align_bytes=64)

        for t in range(PACK):
            nc.vector.tensor_copy(picked_b[0][:, t, :], xb_sb[0][:, t, :].indirect(list_b[:]))
        for a in range(PASSES):
            nc.vector.tensor_copy(
                out=w_plane[:, a].rearrange("p t (c i) -> p c t i", i=16),
                in_=ws_raw[:, a].rearrange("p (c i t) -> p c t i", i=16, t=PACK),
            )

        ident = keep.tile([P, P], F32, name="ident")
        make_identity(nc, ident[:])
        bi_ps = psum.tile([P, 2, P], F32, name="bi_ps")
        for h in range(2):
            nc.tensor.transpose(bi_ps[:, h, :], bi_col[:, h : h + 1].to_broadcast([P, P]), ident[:])
        bi_rows = keep.tile([P, N], F32, name="bi_rows")
        nc.scalar.copy(bi_rows[:].rearrange("p (c h) -> p c h", h=2), bi_ps[:].rearrange("p h c -> p c h"))

        a_ps = [psum.tile([P, J], F32, name="a_ps%d" % t) for t in range(PACK)]

        def multiply(a, t, cols):
            nc.vector.scalar_tensor_tensor(
                out=u_rows[a][:, t, cols],
                in0=picked_a[a][:, t, cols],
                scalar=fk_sb[:, a, t : t + 1],
                in1=picked_b[a][:, t, cols],
                op0=ALU.mult,
                op1=ALU.mult,
            )

        def interleave(copy, dst, a, cols):
            copy(
                dst[:].rearrange("p (c i) t -> p c t i", i=4),
                u_rows[a][:, :, cols].rearrange("p t (c i) -> p c t i", i=4),
            )

        def quantize(src, a, cols):
            nc.vector.quantize_mx(
                out=u_codes[a][:, cols].bitcast(E5M2X4),
                scales=u_plane[a][:, cols],
                in_=src[:].rearrange("p c t -> p (c t)"),
            )

        def deal_w(a, t0, t1, tag):
            dealt = keep.tile([P, t1 - t0, P], I32, name="w_codes%d%d" % (a, t0), tag=tag, align_bytes=64)
            for t in range(t0, t1):
                w_codes[a, t] = dealt[:, t - t0, :]
            nc.vector.tensor_copy(
                out=dealt[:].rearrange("p t (c i) -> p c t i", i=4),
                in_=w_raw[a][:].rearrange("p (c i t) -> p c t i", i=4, t=PACK)[:, :, t0:t1, :],
            )

        def first_product(a):
            for t in range(PACK):
                nc.tensor.matmul_mx(
                    out=a_ps[t][:],
                    lhsT=w_codes[a, t].bitcast(E5M2X4),
                    lhsT_scale=w_plane[:, a, t, :],
                    rhs=u_codes[a][:].bitcast(E5M2X4),
                    rhs_scale=u_plane[a][:],
                    start=(a == 0),
                    stop=(a == PASSES - 1),
                )

        halves = [slice(0, HALF), slice(HALF, J)]
        everything = slice(0, J)
        for g, (a, t0, t1) in enumerate(xa_loads):
            for t in range(t0, t1):
                nc.scalar.activation(picked_a[a][:, t, :], xa_sb[g][:, t - t0, :].indirect(list_a[:]), ACT.Copy)
                multiply(a, t, everything)
            if t1 == PACK:
                interleave(nc.vector.tensor_copy, u_bf, a, everything)
                deal_w(a, 0, PACK, "w_codes")
                quantize(u_bf, a, everything)
                first_product(a)
                u_rows.append(keep.tile([P, PACK, J], F32, name="u_rows1", tag="u_bf", align_bytes=64))
                for t in range(0, 2):
                    nc.scalar.activation(picked_b[1][:, t, :], xb_sb[1][:, t, :].indirect(list_b[:]), ACT.Copy)
                for t in range(2, PACK):
                    nc.vector.tensor_copy(picked_b[1][:, t, :], xb_sb[1][:, t, :].indirect(list_b[:]))
                nc.vector.tensor_scalar(scaled_b[:], picked_b[1][:, PACK - 1, :], fk_sb[:, 1, PACK - 1 : PACK], None, ALU.mult)

        a, t = PASSES - 1, PACK - 1
        picked_last = keep.tile([P, HALF], F32, name="picked_last")
        nc.scalar.activation(picked_last[:], xa_last[:].indirect(list_a[:, LIST_COLS // 2 :]), ACT.Copy)
        nc.vector.tensor_tensor(
            u_rows[a][:, t, halves[0]], xa_last[:].indirect(list_a[:, : LIST_COLS // 2]), scaled_b[:, halves[0]], ALU.mult
        )
        nc.vector.tensor_tensor(u_rows[a][:, t, halves[1]], picked_last[:], scaled_b[:, halves[1]], ALU.mult)
        u_bf_half = [keep.tile([P, HALF, PACK], BF16, name="u_bf_half%d" % h, tag="u_bf_half%d" % h, align_bytes=64) for h in range(2)]
        interleave(nc.scalar.copy, u_bf_half[0], a, halves[0])
        deal_w(a, 0, 2, "scaled_b")
        interleave(nc.vector.tensor_copy, u_bf_half[1], a, halves[1])
        for h in range(2):
            quantize(u_bf_half[h], a, halves[h])
        deal_w(a, 2, PACK, "u_bf_half0")
        first_product(a)

        a_sb = keep.tile([P, PACK, J], F32, name="a_sb")
        peak = keep.tile([P, PACK], F32, name="peak")
        inv_peak = keep.tile([P, PACK], F32, name="inv_peak")
        factor = keep.tile([P, PACK], F32, name="factor")
        for t in range(PACK):
            nc.scalar.copy(a_sb[:, t, :], a_ps[t][:])
            nc.vector.tensor_reduce(peak[:, t : t + 1], a_sb[:, t, :], AXIS_X, ALU.max, apply_absolute_value=True)
        nc.vector.reciprocal(inv_peak[:], peak[:])
        nc.vector.tensor_tensor(factor[:], inv_peak[:], us_sb[:], ALU.mult)

        hid_bf = [keep.tile([P, HALF, PACK], BF16, name="hid_bf%d" % h, align_bytes=64) for h in range(2)]
        hid_codes = [keep.tile([P, HALF], I32, name="hid_codes%d" % h, align_bytes=64) for h in range(2)]
        hid_plane = [keep.tile([P, HALF], U8, name="hid_plane%d" % h, align_bytes=64) for h in range(2)]
        p_ps = [psum.tile([P, N], F32, name="p_ps%d" % h) for h in range(2)]
        factor_spread = factor[:].rearrange("p (c t i) -> p c t i", c=1, i=1).to_broadcast([P, HALF // 4, PACK, 4])
        for h in range(2):
            nc.vector.tensor_tensor(
                hid_bf[h][:].rearrange("p (c i) t -> p c t i", i=4),
                a_sb[:, :, halves[h]].rearrange("p t (c i) -> p c t i", i=4),
                factor_spread,
                ALU.mult,
            )
        for h in range(2):
            nc.vector.quantize_mx(
                out=hid_codes[h][:].bitcast(E5M2X4),
                scales=hid_plane[h][:],
                in_=hid_bf[h][:].rearrange("p c t -> p (c t)"),
            )
            nc.tensor.matmul_mx(
                out=p_ps[h][:],
                lhsT=hid_codes[h][:].bitcast(E5M2X4),
                lhsT_scale=hid_plane[h][:],
                rhs=wb_codes[:].bitcast(E2M1X4),
                rhs_scale=wb_plane[:],
                start=True,
                stop=True,
            )

        neg_z = [keep.tile([P, N], F32, name="neg_z%d" % h) for h in range(2)]
        neg_top = [keep.tile([P, 1], F32, name="neg_top%d" % h) for h in range(2)]
        ea = [keep.tile([P, N], F32, name="ea%d" % h) for h in range(2)]
        total = [keep.tile([P, 1], F32, name="total%d" % h) for h in range(2)]
        inv_total = [keep.tile([P, 1], F32, name="inv_total%d" % h) for h in range(2)]
        shares = [keep.tile([P, N], F32, name="shares%d" % h) for h in range(2)]
        for h in range(2):
            nc.vector.scalar_tensor_tensor(
                out=neg_z[h][:], in0=p_ps[h][:], scalar=-0.7, in1=bi_rows[:], op0=ALU.mult, op1=ALU.subtract
            )
        for h in range(2):
            nc.vector.tensor_reduce(neg_top[h][:], neg_z[h][:], AXIS_X, ALU.min)
            nc.scalar.activation(
                ea[h][:], neg_z[h][:], ACT.Exp, bias=neg_top[h][:], scale=-1.0, accum_out=total[h][:]
            )
        for h in range(2):
            nc.vector.reciprocal(inv_total[h][:], total[h][:])
            nc.vector.tensor_scalar(shares[h][:], ea[h][:], inv_total[h][:], 256.0, ALU.mult, ALU.mult)
            nc.sync.dma_start(out=out[halves[h], :], in_=shares[h][:])
